import numpy as np
import ml_dtypes


def mxq(x, axis, fmt="e4m3"):
    dtype, down = {"e4m3": (ml_dtypes.float8_e4m3fn, 7), "e5m2": (ml_dtypes.float8_e5m2, 14)}[fmt]
    v = np.moveaxis(np.asarray(x, np.float32).astype(ml_dtypes.bfloat16).astype(np.float64), axis, -1)
    blocks = v.reshape(v.shape[:-1] + (-1, 32))
    amax = np.abs(blocks).max(-1, keepdims=True)
    byte = np.maximum(np.where(amax > 0, np.frexp(amax)[1] - 1 + 127, 0) - down, 1)
    scale = np.exp2(byte - 127.0)
    codes = (blocks / scale).astype(np.float32).astype(dtype).astype(np.float64)
    return np.moveaxis((codes * scale).reshape(v.shape), -1, axis)


WIDE = False


def mx_kscale(k):
    if not WIDE:
        return np.ones(k)
    levels = np.array([10, -10, 5, -5, 0])
    if k % 512:
        return np.exp2(np.random.permutation(np.resize(levels, k // 32))).repeat(32)
    a = np.empty((k // 512, 16))
    for p in range(k // 512):
        a[p, :8] = np.random.permutation(np.resize(levels, 8))
        for g in range(8):
            far = levels[np.abs(levels - a[p, g]) >= 10]
            a[p, g + 8] = far[np.random.randint(len(far))]
    return np.exp2(a.ravel()).repeat(32)


def f64(x):
    return np.asarray(x).astype(np.float64)


def striped(idx):
    return np.tile(np.asarray(idx).reshape(-1, 16).T, (8, 1)).astype(np.uint16)


def unstriped(offs):
    return offs[:16].T.reshape(-1).astype(np.int64)


E2M1 = np.array([0.0, 0.5, 1.0, 1.5, 2.0, 3.0, 4.0, 6.0, -0.0, -0.5, -1.0, -1.5, -2.0, -3.0, -4.0, -6.0])


def pack_weight(w, fmt):
    k, n = w.shape
    w = f64(np.asarray(w, np.float32).astype(ml_dtypes.bfloat16)).reshape(k // 32, 32, n)
    amax = np.abs(w).max(1)
    if fmt == "e4m3":
        byte = np.frexp(amax)[1] - 1 + 127 - 7
    else:
        mant, ex = np.frexp(amax / 6.0)
        byte = np.where(mant > 0.5, ex, ex - 1) + 127
    byte = np.clip(np.where(amax > 0, byte, 1), 1, 254)
    scaled = (w * np.exp2(127.0 - byte)[:, None, :]).reshape(k, n).astype(np.float32)
    by_word = np.ascontiguousarray(scaled.reshape(k // 512, 128, 4, n).transpose(0, 1, 3, 2))
    if fmt == "e4m3":
        words = by_word.astype(ml_dtypes.float8_e4m3fn).view(np.uint8)
    else:
        c = by_word.astype(ml_dtypes.float4_e2m1fn).view(np.uint8) & 0xF
        words = (c[..., 0::2] | (c[..., 1::2] << 4)).reshape(k // 512, 128, 2 * n)
    return np.ascontiguousarray(words), np.ascontiguousarray(byte.astype(np.uint8).reshape(k // 512, 16, n))


def unpack_weight(words, scales, fmt):
    g, _, n = scales.shape
    words = np.ascontiguousarray(words).reshape(g, 128, n, -1)
    if fmt == "e4m3":
        vals = words.view(ml_dtypes.float8_e4m3fn).astype(np.float64)
    else:
        nib = np.empty((g, 128, n, 4), np.uint8)
        nib[..., 0::2] = words & 0xF
        nib[..., 1::2] = words >> 4
        vals = E2M1[nib]
    vals = vals * np.repeat(np.exp2(scales.astype(np.float64) - 127.0), 8, axis=1)[..., None]
    return vals.transpose(0, 1, 3, 2).reshape(g * 512, n)


def sigmoid(v):
    return 1.0 / (1.0 + np.exp(-v))


D, T, I, Q, E = 512, 2048, 512, 128, 512


def setup_inputs():
    n = np.random.standard_normal
    idx = np.random.permutation(T)[:I]
    idx2 = np.random.permutation(T)[:I]
    idx3 = np.random.permutation(T)[:I]
    fd = mx_kscale(D)
    fi = mx_kscale(I)
    ti = np.ones(T)
    ti[idx] = fi
    keysp = pack_weight(n((D, T)) / fd[:, None], "e2m1")
    return {
        "query": (n((D, Q)) * 0.9 / np.sqrt(D) * fd[:, None]).astype(np.float32),
        "keys_words": keysp[0],
        "keys_scales": keysp[1],
        "lam": (np.random.uniform(0.3, 0.9, (Q, 1))).astype(np.float32),
        "damp": (np.random.uniform(1.0, 4.0, (Q, 1))).astype(np.float32),
        "os": (np.random.uniform(4.0, 16.0, (1, I)) * fi).astype(np.float32),
        "vals": (n((E, T)) / ti).astype(np.float32),
        "before": (n((Q, E)) * 1.0).astype(np.float32),
        "eager2": (np.random.uniform(0.5, 1.5, (Q, 1))).astype(np.float32),
        "offs": striped(idx),
        "offs2": striped(idx2),
        "offs3": striped(idx3),
    }


def reference(query, keys_words, keys_scales, lam, damp, os, vals, before, eager2, offs, offs2, offs3):
    idx = unstriped(offs)
    idx2 = unstriped(offs2)
    idx3 = unstriped(offs3)
    keysu = unpack_weight(keys_words, keys_scales, "e2m1")
    queryq = mxq(f64(query), 0, "e4m3")
    a = queryq.T @ keysu
    s = a[:, idx] + np.maximum(a[:, idx2], a[:, idx3]) * f64(lam)
    p = np.exp(s - np.max(s, axis=1, keepdims=True))
    r = p / np.sum(p, axis=1, keepdims=True) * 512.0
    u0 = np.log(r * f64(damp) + 1.0)
    w = u0 / np.sum(u0, axis=1, keepdims=True)
    wo1 = w * f64(os)
    wt1 = wo1.T
    vt1 = f64(vals)[:, idx].T
    wt1q = mxq(wt1, 0, "e4m3")
    vt1q = mxq(vt1, 0, "e4m3")
    o = wt1q.T @ vt1q
    df0 = o - f64(before)
    gt1 = sigmoid(np.mean(np.square(df0), axis=1, keepdims=True) * f64(eager2) - 1.0)
    y = f64(before) + df0 * gt1
    return y

@@ -1,0 +1,223 @@
+from contextlib import ExitStack
+
+import concourse.mybir as mybir
+from concourse.masks import make_identity
+
+D, T, I, Q, E = 512, 2048, 512, 128, 512
+FLOPS = 2 * D * Q * T + 2 * I * Q * E
+
+F32 = mybir.dt.float32
+BF16 = mybir.dt.bfloat16
+I32 = mybir.dt.int32
+U32 = mybir.dt.uint32
+U16 = mybir.dt.uint16
+U8 = mybir.dt.uint8
+FP8X4 = mybir.dt.float8_e4m3fn_x4
+FP4X4 = mybir.dt.float4_e2m1fn_x4
+ALU = mybir.AluOpType
+ACT = mybir.ActivationFunctionType
+AXIS_X = mybir.AxisListType.X
+
+P = 128
+PACK = 4
+BANK = 512
+HALF = E // 2
+
+
+def tile_attend_lookahead_dampened_movedbychange_kernel(
+    tc, query, keys_words, keys_scales, lam, damp, slot_factor, vals, before, eager2, offs, offs2, offs3, out
+):
+    nc = tc.nc
+    with ExitStack() as ctx:
+        sb = ctx.enter_context(tc.tile_pool(name="sb", bufs=1))
+        ps = ctx.enter_context(tc.psum_pool(name="ps", bufs=1))
+
+        def column(name, src):
+            col = sb.tile([P, 1], F32, name=name)
+            nc.sync.dma_start(col[:], src)
+            return col
+
+        def offsets(name, src):
+            lst = sb.tile([P, I // 16], U16, name=name)
+            nc.sync.dma_start(lst[:], src)
+            return lst
+
+        def value_block(b):
+            blk = sb.tile([P, T], F32, name="vals%d" % b)
+            nc.sync.dma_start(blk[:], vals[b * P : (b + 1) * P, :])
+            return blk
+
+        q_raw = sb.tile([P, PACK, Q], F32)
+        nc.sync.dma_start(q_raw[:], query.rearrange("(p j) w -> p j w", j=PACK))
+        k_words = sb.tile([P, 2 * T], U8, align_bytes=64)
+        nc.sync.dma_start(k_words[:].bitcast(I32), keys_words[0].bitcast(I32))
+        k_scales = sb.tile([P, T], U8, align_bytes=64)
+        nc.vector.memset(k_scales[:].bitcast(I32), 0)
+        for g in range(4):
+            nc.sync.dma_start(
+                k_scales[32 * g : 32 * g + 4, :].bitcast(I32),
+                keys_scales[0, 4 * g : 4 * g + 4, :].bitcast(I32),
+            )
+        v_pool = [value_block(0)]
+        list1 = offsets("list1", offs)
+        list2 = offsets("list2", offs2)
+        list3 = offsets("list3", offs3)
+        v_pool.append(value_block(1))
+        lam_col = column("lam_col", lam)
+        os_cols = sb.tile([P, PACK], F32)
+        nc.sync.dma_start(os_cols[:], slot_factor.rearrange("o (p t) -> p (o t)", t=PACK))
+        damp_col = column("damp_col", damp)
+        v_pool.append(value_block(2))
+        eager_col = column("eager_col", eager2)
+        v_pool.append(value_block(3))
+        before_sb = sb.tile([P, E], F32)
+        nc.sync.dma_start(before_sb[:], before)
+
+        ident = sb.tile([P, P], F32)
+        make_identity(nc, ident[:])
+
+        q_grouped = sb.tile([P, Q, PACK], BF16, align_bytes=64)
+        nc.vector.tensor_copy(q_grouped[:], q_raw[:].rearrange("p j w -> p w j"))
+        q_codes = sb.tile([P, Q], U32, align_bytes=64)
+        q_scales = sb.tile([P, Q], U8, align_bytes=64)
+        nc.vector.quantize_mx(
+            out=q_codes[:].bitcast(FP8X4), scales=q_scales[:], in_=q_grouped[:].rearrange("p w j -> p (w j)")
+        )
+        a = sb.tile([P, T], F32)
+        for c in range(T // BANK):
+            cols = slice(c * BANK, (c + 1) * BANK)
+            a_bank = ps.tile([P, BANK], F32, name="a_bank%d" % c, tag="bank%d" % c)
+            nc.tensor.matmul_mx(
+                out=a_bank[:],
+                lhsT=q_codes[:].bitcast(FP8X4),
+                lhsT_scale=q_scales[:],
+                rhs=k_words[:, 2 * c * BANK : 2 * (c + 1) * BANK].bitcast(FP4X4),
+                rhs_scale=k_scales[:, cols],
+                start=True,
+                stop=True,
+            )
+            nc.vector.tensor_copy(a[:, cols], a_bank[:])
+
+        os_bank = ps.tile([P, PACK, P], F32, tag="bank4")
+        for t in range(PACK):
+            nc.tensor.transpose(os_bank[:, t, :], os_cols[:, t : t + 1].to_broadcast([P, P]), ident[:])
+
+        v_grouped = sb.tile([P, E, PACK], BF16, align_bytes=64)
+        v_codes = sb.tile([P, E], U32, align_bytes=64)
+        v_scales = sb.tile([P, E], U8, align_bytes=64)
+
+        def turn(src, bank):
+            words = src.bitcast(F32)
+            for u in range(2):
+                nc.tensor.transpose(bank[:, u, :], words[:, u : I // 2 : 2], ident[:])
+
+        def weave(dst, bank, on_scalar):
+            if on_scalar:
+                nc.scalar.copy(dst.bitcast(F32), bank[:].rearrange("p u c -> p c u"))
+            else:
+                nc.vector.tensor_copy(dst.bitcast(F32), bank[:].rearrange("p u c -> p c u"))
+
+        def pick_values(b, on_scalar):
+            picked = sb.tile([P, I], BF16, name="picked%d" % b)
+            if on_scalar:
+                nc.scalar.activation(picked[:], v_pool[b][:].indirect(list1[:]), ACT.Copy)
+            else:
+                nc.vector.tensor_copy(picked[:], v_pool[b][:].indirect(list1[:]))
+            v_bank = ps.tile([P, 2, P], F32, name="v_bank%d" % b, tag="bank%d" % b)
+            turn(picked[:], v_bank)
+            return v_bank
+
+        def weave_values(b, v_bank, on_scalar):
+            weave(v_grouped[:, b * P : (b + 1) * P, :], v_bank, on_scalar)
+
+        def quantize_values(h):
+            cols = slice(h * HALF, (h + 1) * HALF)
+            nc.vector.quantize_mx(
+                out=v_codes[:, cols].bitcast(FP8X4),
+                scales=v_scales[:, cols],
+                in_=v_grouped[:, cols, :].rearrange("p e j -> p (e j)"),
+            )
+
+        v_bank0 = pick_values(0, True)
+
+        a2 = sb.tile([P, I], F32)
+        nc.scalar.activation(a2[:], a[:].indirect(list2[:]), ACT.Copy)
+        a3 = sb.tile([P, I], F32)
+        nc.vector.tensor_copy(a3[:], a[:].indirect(list3[:]))
+        a1 = sb.tile([P, I], F32)
+        nc.scalar.activation(a1[:], a[:].indirect(list1[:]), ACT.Copy)
+        follow = sb.tile([P, I], F32)
+        nc.vector.tensor_tensor(follow[:], a2[:], a3[:], ALU.max)
+        weave_values(0, v_bank0, False)
+        s = sb.tile([P, I], F32)
+        nc.vector.scalar_tensor_tensor(s[:], follow[:], lam_col[:], a1[:], ALU.mult, ALU.add)
+        neg_max = sb.tile([P, 1], F32)
+        nc.vector.tensor_reduce(neg_max[:], s[:], AXIS_X, ALU.max, negate=True)
+        v_bank1 = pick_values(1, True)
+
+        p = sb.tile([P, I], F32)
+        p_sum = sb.tile([P, 1], F32)
+        nc.scalar.activation(p[:], s[:], ACT.Exp, bias=neg_max[:], accum_out=p_sum[:])
+        v_bank2 = pick_values(2, False)
+        p_inv = sb.tile([P, 1], F32)
+        nc.vector.reciprocal(p_inv[:], p_sum[:])
+        gain = sb.tile([P, 1], F32)
+        nc.vector.tensor_scalar(gain[:], p_inv[:], damp_col[:], float(I), ALU.mult, ALU.mult)
+        u0 = sb.tile([P, I], F32)
+        u_sum = sb.tile([P, 1], F32)
+        nc.scalar.activation(u0[:], p[:], ACT.Ln, bias=1.0, scale=gain[:], accum_out=u_sum[:])
+
+        weave_values(1, v_bank1, False)
+        v_bank3 = pick_values(3, False)
+        quantize_values(0)
+        eager_mean = sb.tile([P, 1], F32)
+        nc.vector.tensor_scalar(eager_mean[:], eager_col[:], 1.0 / E, None, ALU.mult)
+        weave_values(2, v_bank2, True)
+        weave_values(3, v_bank3, True)
+
+        u_inv = sb.tile([P, 1], F32)
+        nc.vector.reciprocal(u_inv[:], u_sum[:])
+        wo = sb.tile([P, I], BF16)
+        nc.vector.scalar_tensor_tensor(
+            wo[:].rearrange("p (s t) -> p s t", t=PACK),
+            u0[:].rearrange("p (s t) -> p s t", t=PACK),
+            u_inv[:],
+            os_bank[:].rearrange("p t s -> p s t"),
+            ALU.mult,
+            ALU.mult,
+        )
+        w_bank = ps.tile([P, 2, P], F32, tag="bank5")
+        turn(wo[:], w_bank)
+        quantize_values(1)
+        w_grouped = sb.tile([P, Q, PACK], BF16, align_bytes=64)
+        weave(w_grouped[:], w_bank, False)
+        w_codes = sb.tile([P, Q], U32, align_bytes=64)
+        w_scales = sb.tile([P, Q], U8, align_bytes=64)
+        nc.vector.quantize_mx(
+            out=w_codes[:].bitcast(FP8X4), scales=w_scales[:], in_=w_grouped[:].rearrange("p w j -> p (w j)")
+        )
+
+        df = sb.tile([P, E], F32)
+        for h in range(2):
+            cols = slice(h * HALF, (h + 1) * HALF)
+            o_bank = ps.tile([P, HALF], F32, name="o_bank%d" % h, tag="bank%d" % (6 + h))
+            nc.tensor.matmul_mx(
+                out=o_bank[:],
+                lhsT=w_codes[:].bitcast(FP8X4),
+                lhsT_scale=w_scales[:],
+                rhs=v_codes[:, cols].bitcast(FP8X4),
+                rhs_scale=v_scales[:, cols],
+                start=True,
+                stop=True,
+            )
+            nc.vector.tensor_tensor(df[:, cols], o_bank[:], before_sb[:, cols], ALU.subtract)
+        sq = sb.tile([P, E], F32)
+        sq_sum = sb.tile([P, 1], F32)
+        nc.vector.scalar_tensor_tensor(sq[:], df[:], 1.0, df[:], ALU.mult, ALU.mult, accum_out=sq_sum[:])
+        gate = sb.tile([P, 1], F32)
+        nc.scalar.activation(gate[:], sq_sum[:], ACT.Sigmoid, bias=-1.0, scale=eager_mean[:])
+        y = sb.tile([P, E], F32)
+        for h in range(2):
+            cols = slice(h * HALF, (h + 1) * HALF)
+            nc.vector.scalar_tensor_tensor(y[:, cols], df[:, cols], gate[:], before_sb[:, cols], ALU.mult, ALU.add)
+            (nc.sync, nc.scalar)[h].dma_start(out[:, cols], y[:, cols])

@@ -22,6 +22,7 @@ P = 128
 PACK = 4
 BANK = 512
 HALF = E // 2
+SCORE_WIDTHS = (512, 512, 512, 512)
 
 
 def tile_attend_lookahead_dampened_movedbychange_kernel(
@@ -43,7 +44,7 @@ def tile_attend_lookahead_dampened_movedbychange_kernel(
             return lst
 
         def value_block(b):
-            blk = sb.tile([P, T], F32, name="vals%d" % b)
+            blk = sb.tile([P, T], F32, name="vals%d" % b, tag="vals%d" % b, align_bytes=64)
             nc.sync.dma_start(blk[:], vals[b * P : (b + 1) * P, :])
             return blk
 
@@ -58,6 +59,7 @@ def tile_attend_lookahead_dampened_movedbychange_kernel(
                 k_scales[32 * g : 32 * g + 4, :].bitcast(I32),
                 keys_scales[0, 4 * g : 4 * g + 4, :].bitcast(I32),
             )
+        eager_col = column("eager_col", eager2)
         v_pool = [value_block(0)]
         list1 = offsets("list1", offs)
         list2 = offsets("list2", offs2)
@@ -68,13 +70,15 @@ def tile_attend_lookahead_dampened_movedbychange_kernel(
         nc.sync.dma_start(os_cols[:], slot_factor.rearrange("o (p t) -> p (o t)", t=PACK))
         damp_col = column("damp_col", damp)
         v_pool.append(value_block(2))
-        eager_col = column("eager_col", eager2)
         v_pool.append(value_block(3))
         before_sb = sb.tile([P, E], F32)
         nc.sync.dma_start(before_sb[:], before)
 
         ident = sb.tile([P, P], F32)
         make_identity(nc, ident[:])
+
+        eager_mean = sb.tile([P, 1], F32)
+        nc.scalar.activation(eager_mean[:], eager_col[:], ACT.Copy, scale=1.0 / E)
 
         q_grouped = sb.tile([P, Q, PACK], BF16, align_bytes=64)
         nc.vector.tensor_copy(q_grouped[:], q_raw[:].rearrange("p j w -> p w j"))
@@ -83,28 +87,25 @@ def tile_attend_lookahead_dampened_movedbychange_kernel(
         nc.vector.quantize_mx(
             out=q_codes[:].bitcast(FP8X4), scales=q_scales[:], in_=q_grouped[:].rearrange("p w j -> p (w j)")
         )
-        a = sb.tile([P, T], F32)
-        for c in range(T // BANK):
-            cols = slice(c * BANK, (c + 1) * BANK)
-            a_bank = ps.tile([P, BANK], F32, name="a_bank%d" % c, tag="bank%d" % c)
+        a = sb.tile([P, T], F32, tag="scores", align_bytes=64)
+        start = 0
+        for c, width in enumerate(SCORE_WIDTHS):
+            cols = slice(start, start + width)
+            a_bank = ps.tile([P, width], F32, name="a_bank%d" % c, tag="bank%d" % c)
             nc.tensor.matmul_mx(
                 out=a_bank[:],
                 lhsT=q_codes[:].bitcast(FP8X4),
                 lhsT_scale=q_scales[:],
-                rhs=k_words[:, 2 * c * BANK : 2 * (c + 1) * BANK].bitcast(FP4X4),
+                rhs=k_words[:, 2 * start : 2 * (start + width)].bitcast(FP4X4),
                 rhs_scale=k_scales[:, cols],
                 start=True,
                 stop=True,
             )
             nc.vector.tensor_copy(a[:, cols], a_bank[:])
+            start += width
 
-        os_bank = ps.tile([P, PACK, P], F32, tag="bank4")
-        for t in range(PACK):
-            nc.tensor.transpose(os_bank[:, t, :], os_cols[:, t : t + 1].to_broadcast([P, P]), ident[:])
-
-        v_grouped = sb.tile([P, E, PACK], BF16, align_bytes=64)
-        v_codes = sb.tile([P, E], U32, align_bytes=64)
-        v_scales = sb.tile([P, E], U8, align_bytes=64)
+        slot_halves = [slice(h * I // 2, (h + 1) * I // 2) for h in range(2)]
+        list_halves = [slice(h * I // 32, (h + 1) * I // 32) for h in range(2)]
 
         def turn(src, bank):
             words = src.bitcast(F32)
@@ -117,78 +118,100 @@ def tile_attend_lookahead_dampened_movedbychange_kernel(
             else:
                 nc.vector.tensor_copy(dst.bitcast(F32), bank[:].rearrange("p u c -> p c u"))
 
-        def pick_values(b, on_scalar):
-            picked = sb.tile([P, I], BF16, name="picked%d" % b)
+        def gather(dst, window, entries, on_scalar):
             if on_scalar:
-                nc.scalar.activation(picked[:], v_pool[b][:].indirect(list1[:]), ACT.Copy)
+                nc.scalar.activation(dst, window[:].indirect(entries), ACT.Copy)
             else:
-                nc.vector.tensor_copy(picked[:], v_pool[b][:].indirect(list1[:]))
+                nc.vector.tensor_copy(dst, window[:].indirect(entries))
+
+        def turn_values(b, picked):
             v_bank = ps.tile([P, 2, P], F32, name="v_bank%d" % b, tag="bank%d" % b)
             turn(picked[:], v_bank)
             return v_bank
 
-        def weave_values(b, v_bank, on_scalar):
-            weave(v_grouped[:, b * P : (b + 1) * P, :], v_bank, on_scalar)
+        def pick_values(b, on_scalar, tag):
+            picked = sb.tile([P, I], BF16, name="picked%d" % b, tag=tag, align_bytes=64)
+            gather(picked[:], v_pool[b], list1[:], on_scalar)
+            return turn_values(b, picked)
 
-        def quantize_values(h):
+        def quantize_values(h, grouped):
             cols = slice(h * HALF, (h + 1) * HALF)
             nc.vector.quantize_mx(
                 out=v_codes[:, cols].bitcast(FP8X4),
                 scales=v_scales[:, cols],
-                in_=v_grouped[:, cols, :].rearrange("p e j -> p (e j)"),
+                in_=grouped[:].rearrange("p e j -> p (e j)"),
             )
 
-        v_bank0 = pick_values(0, True)
-
-        a2 = sb.tile([P, I], F32)
-        nc.scalar.activation(a2[:], a[:].indirect(list2[:]), ACT.Copy)
-        a3 = sb.tile([P, I], F32)
-        nc.vector.tensor_copy(a3[:], a[:].indirect(list3[:]))
+        v_banks = [pick_values(0, True, "picked0")]
         a1 = sb.tile([P, I], F32)
-        nc.scalar.activation(a1[:], a[:].indirect(list1[:]), ACT.Copy)
-        follow = sb.tile([P, I], F32)
-        nc.vector.tensor_tensor(follow[:], a2[:], a3[:], ALU.max)
-        weave_values(0, v_bank0, False)
+        a2 = sb.tile([P, I], F32, tag="vals0", align_bytes=64)
+        a3 = sb.tile([P, I], F32)
+        for h in range(2):
+            gather(a2[:, slot_halves[h]], a, list2[:, list_halves[h]], True)
+            gather(a1[:, slot_halves[h]], a, list1[:, list_halves[h]], True)
+            gather(a3[:, slot_halves[h]], a, list3[:, list_halves[h]], False)
+        follow = sb.tile([P, I], F32, tag="follow", align_bytes=64)
         s = sb.tile([P, I], F32)
-        nc.vector.scalar_tensor_tensor(s[:], follow[:], lam_col[:], a1[:], ALU.mult, ALU.add)
+        lo, hi = slot_halves
+        nc.vector.tensor_tensor(follow[:, lo], a2[:, lo], a3[:, lo], ALU.max)
+        nc.vector.scalar_tensor_tensor(s[:, lo], follow[:, lo], lam_col[:], a1[:, lo], ALU.mult, ALU.add)
+        nc.vector.tensor_tensor(follow[:, hi], a2[:, hi], a3[:, hi], ALU.max)
+        neg_max_lo = sb.tile([P, 1], F32)
+        nc.vector.tensor_reduce(neg_max_lo[:], s[:, lo], AXIS_X, ALU.max, negate=True)
+        nc.vector.scalar_tensor_tensor(s[:, hi], follow[:, hi], lam_col[:], a1[:, hi], ALU.mult, ALU.add)
         neg_max = sb.tile([P, 1], F32)
-        nc.vector.tensor_reduce(neg_max[:], s[:], AXIS_X, ALU.max, negate=True)
-        v_bank1 = pick_values(1, True)
+        nc.vector.tensor_scalar(
+            follow[:, hi], s[:, hi], -1.0, neg_max_lo[:], ALU.mult, ALU.min, accum_out=neg_max[:]
+        )
+        v_banks.append(pick_values(1, True, "scores"))
+        os_bank = ps.tile([P, PACK, P], F32, tag="bank4")
+        for t in range(PACK):
+            nc.tensor.transpose(os_bank[:, t, :], os_cols[:, t : t + 1].to_broadcast([P, P]), ident[:])
 
-        p = sb.tile([P, I], F32)
-        p_sum = sb.tile([P, 1], F32)
+        p = sb.tile([P, I], F32, tag="vals1", align_bytes=64)
+        p_sum = sb.tile([P, 1], F32, tag="p_sum", align_bytes=64)
         nc.scalar.activation(p[:], s[:], ACT.Exp, bias=neg_max[:], accum_out=p_sum[:])
-        v_bank2 = pick_values(2, False)
-        p_inv = sb.tile([P, 1], F32)
+        v_banks.append(pick_values(2, False, "follow"))
+        p_inv = sb.tile([P, 1], F32, tag="vals2", align_bytes=64)
         nc.vector.reciprocal(p_inv[:], p_sum[:])
-        gain = sb.tile([P, 1], F32)
+        gain = sb.tile([P, 1], F32, tag="gain", align_bytes=64)
         nc.vector.tensor_scalar(gain[:], p_inv[:], damp_col[:], float(I), ALU.mult, ALU.mult)
         u0 = sb.tile([P, I], F32)
         u_sum = sb.tile([P, 1], F32)
         nc.scalar.activation(u0[:], p[:], ACT.Ln, bias=1.0, scale=gain[:], accum_out=u_sum[:])
 
-        weave_values(1, v_bank1, False)
-        v_bank3 = pick_values(3, False)
-        quantize_values(0)
-        eager_mean = sb.tile([P, 1], F32)
-        nc.vector.tensor_scalar(eager_mean[:], eager_col[:], 1.0 / E, None, ALU.mult)
-        weave_values(2, v_bank2, True)
-        weave_values(3, v_bank3, True)
+        picked3 = sb.tile([P, I], BF16, tag="p_sum", align_bytes=64)
+        for h in range(2):
+            gather(picked3[:, slot_halves[h]], v_pool[3], list1[:, list_halves[h]], False)
+        v_banks.append(turn_values(3, picked3))
+        v_grouped = []
+        for h, tag in enumerate(("gain", "vals1")):
+            grouped = sb.tile([P, HALF, PACK], BF16, name="v_grouped%d" % h, tag=tag, align_bytes=64)
+            for b in range(2):
+                weave(grouped[:, b * P : (b + 1) * P, :], v_banks[2 * h + b], True)
+            v_grouped.append(grouped)
 
-        u_inv = sb.tile([P, 1], F32)
+        table_warm_up = sb.tile([P, 1], F32)
+        nc.scalar.activation(table_warm_up[:], v_grouped[1][:, HALF - 1, 0:1], ACT.Sigmoid)
+        u_inv = sb.tile([P, 1], F32, tag="vals3", align_bytes=64)
         nc.vector.reciprocal(u_inv[:], u_sum[:])
-        wo = sb.tile([P, I], BF16)
-        nc.vector.scalar_tensor_tensor(
-            wo[:].rearrange("p (s t) -> p s t", t=PACK),
-            u0[:].rearrange("p (s t) -> p s t", t=PACK),
-            u_inv[:],
-            os_bank[:].rearrange("p t s -> p s t"),
-            ALU.mult,
-            ALU.mult,
-        )
         w_bank = ps.tile([P, 2, P], F32, tag="bank5")
-        turn(wo[:], w_bank)
-        quantize_values(1)
+        for u in range(2):
+            places = slice(2 * u, 2 * u + 2)
+            wo = sb.tile([P, P, 2], BF16, name="wo%d" % u)
+            nc.vector.scalar_tensor_tensor(
+                wo[:],
+                u0[:].rearrange("p (s t) -> p s t", t=PACK)[:, :, places],
+                u_inv[:],
+                os_bank[:, places, :].rearrange("p t s -> p s t"),
+                ALU.mult,
+                ALU.mult,
+            )
+            nc.tensor.transpose(w_bank[:, u, :], wo[:].rearrange("p s j -> p (s j)").bitcast(F32), ident[:])
+        v_codes = sb.tile([P, E], U32, tag="vals3", align_bytes=64)
+        v_scales = sb.tile([P, E], U8, align_bytes=64)
+        quantize_values(0, v_grouped[0])
+        quantize_values(1, v_grouped[1])
         w_grouped = sb.tile([P, Q, PACK], BF16, align_bytes=64)
         weave(w_grouped[:], w_bank, False)
         w_codes = sb.tile([P, Q], U32, align_bytes=64)
@@ -212,10 +235,14 @@ def tile_attend_lookahead_dampened_movedbychange_kernel(
             )
             nc.vector.tensor_tensor(df[:, cols], o_bank[:], before_sb[:, cols], ALU.subtract)
         sq = sb.tile([P, E], F32)
-        sq_sum = sb.tile([P, 1], F32)
-        nc.vector.scalar_tensor_tensor(sq[:], df[:], 1.0, df[:], ALU.mult, ALU.mult, accum_out=sq_sum[:])
+        sq_lo = sb.tile([P, 1], F32)
+        nc.scalar.activation(sq[:, :HALF], df[:, :HALF], ACT.Square, accum_out=sq_lo[:])
+        sq_hi = sb.tile([P, 1], F32)
+        nc.scalar.activation(sq[:, HALF:], df[:, HALF:], ACT.Square, accum_out=sq_hi[:])
+        gate_bias = sb.tile([P, 1], F32)
+        nc.vector.tensor_scalar(gate_bias[:], sq_lo[:], eager_mean[:], -1.0, ALU.mult, ALU.add)
         gate = sb.tile([P, 1], F32)
-        nc.scalar.activation(gate[:], sq_sum[:], ACT.Sigmoid, bias=-1.0, scale=eager_mean[:])
+        nc.scalar.activation(gate[:], sq_hi[:], ACT.Sigmoid, bias=gate_bias[:], scale=eager_mean[:])
         y = sb.tile([P, E], F32)
         for h in range(2):
             cols = slice(h * HALF, (h + 1) * HALF)

from contextlib import ExitStack

import concourse.mybir as mybir
from concourse.masks import make_identity

D, T, I, Q, E = 512, 2048, 512, 128, 512
FLOPS = 2 * D * Q * T + 2 * I * Q * E

F32 = mybir.dt.float32
BF16 = mybir.dt.bfloat16
I32 = mybir.dt.int32
U32 = mybir.dt.uint32
U16 = mybir.dt.uint16
U8 = mybir.dt.uint8
FP8X4 = mybir.dt.float8_e4m3fn_x4
FP4X4 = mybir.dt.float4_e2m1fn_x4
ALU = mybir.AluOpType
ACT = mybir.ActivationFunctionType
AXIS_X = mybir.AxisListType.X

P = 128
PACK = 4
BANK = 512
HALF = E // 2
SCORE_WIDTHS = (512, 512, 512, 512)


def tile_attend_lookahead_dampened_movedbychange_kernel(
    tc, query, keys_words, keys_scales, lam, damp, slot_factor, vals, before, eager2, offs, offs2, offs3, out
):
    nc = tc.nc
    with ExitStack() as ctx:
        sb = ctx.enter_context(tc.tile_pool(name="sb", bufs=1))
        ps = ctx.enter_context(tc.psum_pool(name="ps", bufs=1))

        def column(name, src):
            col = sb.tile([P, 1], F32, name=name)
            nc.sync.dma_start(col[:], src)
            return col

        def offsets(name, src):
            lst = sb.tile([P, I // 16], U16, name=name)
            nc.sync.dma_start(lst[:], src)
            return lst

        def value_block(b):
            blk = sb.tile([P, T], F32, name="vals%d" % b, tag="vals%d" % b, align_bytes=64)
            nc.sync.dma_start(blk[:], vals[b * P : (b + 1) * P, :])
            return blk

        q_raw = sb.tile([P, PACK, Q], F32)
        nc.sync.dma_start(q_raw[:], query.rearrange("(p j) w -> p j w", j=PACK))
        k_words = sb.tile([P, 2 * T], U8, align_bytes=64)
        nc.sync.dma_start(k_words[:].bitcast(I32), keys_words[0].bitcast(I32))
        k_scales = sb.tile([P, T], U8, align_bytes=64)
        nc.vector.memset(k_scales[:].bitcast(I32), 0)
        for g in range(4):
            nc.sync.dma_start(
                k_scales[32 * g : 32 * g + 4, :].bitcast(I32),
                keys_scales[0, 4 * g : 4 * g + 4, :].bitcast(I32),
            )
        eager_col = column("eager_col", eager2)
        v_pool = [value_block(0)]
        list1 = offsets("list1", offs)
        list2 = offsets("list2", offs2)
        list3 = offsets("list3", offs3)
        v_pool.append(value_block(1))
        lam_col = column("lam_col", lam)
        os_cols = sb.tile([P, PACK], F32)
        nc.sync.dma_start(os_cols[:], slot_factor.rearrange("o (p t) -> p (o t)", t=PACK))
        damp_col = column("damp_col", damp)
        v_pool.append(value_block(2))
        v_pool.append(value_block(3))
        before_sb = sb.tile([P, E], F32)
        nc.sync.dma_start(before_sb[:], before)

        ident = sb.tile([P, P], F32)
        make_identity(nc, ident[:])

        eager_mean = sb.tile([P, 1], F32)
        nc.scalar.activation(eager_mean[:], eager_col[:], ACT.Copy, scale=1.0 / E)

        q_grouped = sb.tile([P, Q, PACK], BF16, align_bytes=64)
        nc.vector.tensor_copy(q_grouped[:], q_raw[:].rearrange("p j w -> p w j"))
        q_codes = sb.tile([P, Q], U32, align_bytes=64)
        q_scales = sb.tile([P, Q], U8, align_bytes=64)
        nc.vector.quantize_mx(
            out=q_codes[:].bitcast(FP8X4), scales=q_scales[:], in_=q_grouped[:].rearrange("p w j -> p (w j)")
        )
        a = sb.tile([P, T], F32, tag="scores", align_bytes=64)
        start = 0
        for c, width in enumerate(SCORE_WIDTHS):
            cols = slice(start, start + width)
            a_bank = ps.tile([P, width], F32, name="a_bank%d" % c, tag="bank%d" % c)
            nc.tensor.matmul_mx(
                out=a_bank[:],
                lhsT=q_codes[:].bitcast(FP8X4),
                lhsT_scale=q_scales[:],
                rhs=k_words[:, 2 * start : 2 * (start + width)].bitcast(FP4X4),
                rhs_scale=k_scales[:, cols],
                start=True,
                stop=True,
            )
            nc.vector.tensor_copy(a[:, cols], a_bank[:])
            start += width

        slot_halves = [slice(h * I // 2, (h + 1) * I // 2) for h in range(2)]
        list_halves = [slice(h * I // 32, (h + 1) * I // 32) for h in range(2)]

        def turn(src, bank):
            words = src.bitcast(F32)
            for u in range(2):
                nc.tensor.transpose(bank[:, u, :], words[:, u : I // 2 : 2], ident[:])

        def weave(dst, bank, on_scalar):
            if on_scalar:
                nc.scalar.copy(dst.bitcast(F32), bank[:].rearrange("p u c -> p c u"))
            else:
                nc.vector.tensor_copy(dst.bitcast(F32), bank[:].rearrange("p u c -> p c u"))

        def gather(dst, window, entries, on_scalar):
            if on_scalar:
                nc.scalar.activation(dst, window[:].indirect(entries), ACT.Copy)
            else:
                nc.vector.tensor_copy(dst, window[:].indirect(entries))

        def turn_values(b, picked):
            v_bank = ps.tile([P, 2, P], F32, name="v_bank%d" % b, tag="bank%d" % b)
            turn(picked[:], v_bank)
            return v_bank

        def pick_values(b, on_scalar, tag):
            picked = sb.tile([P, I], BF16, name="picked%d" % b, tag=tag, align_bytes=64)
            gather(picked[:], v_pool[b], list1[:], on_scalar)
            return turn_values(b, picked)

        def quantize_values(h, grouped):
            cols = slice(h * HALF, (h + 1) * HALF)
            nc.vector.quantize_mx(
                out=v_codes[:, cols].bitcast(FP8X4),
                scales=v_scales[:, cols],
                in_=grouped[:].rearrange("p e j -> p (e j)"),
            )

        v_banks = [pick_values(0, True, "picked0")]
        a1 = sb.tile([P, I], F32)
        a2 = sb.tile([P, I], F32, tag="vals0", align_bytes=64)
        a3 = sb.tile([P, I], F32)
        for h in range(2):
            gather(a2[:, slot_halves[h]], a, list2[:, list_halves[h]], True)
            gather(a1[:, slot_halves[h]], a, list1[:, list_halves[h]], True)
            gather(a3[:, slot_halves[h]], a, list3[:, list_halves[h]], False)
        follow = sb.tile([P, I], F32, tag="follow", align_bytes=64)
        s = sb.tile([P, I], F32)
        lo, hi = slot_halves
        nc.vector.tensor_tensor(follow[:, lo], a2[:, lo], a3[:, lo], ALU.max)
        nc.vector.scalar_tensor_tensor(s[:, lo], follow[:, lo], lam_col[:], a1[:, lo], ALU.mult, ALU.add)
        nc.vector.tensor_tensor(follow[:, hi], a2[:, hi], a3[:, hi], ALU.max)
        neg_max_lo = sb.tile([P, 1], F32)
        nc.vector.tensor_reduce(neg_max_lo[:], s[:, lo], AXIS_X, ALU.max, negate=True)
        nc.vector.scalar_tensor_tensor(s[:, hi], follow[:, hi], lam_col[:], a1[:, hi], ALU.mult, ALU.add)
        neg_max = sb.tile([P, 1], F32)
        nc.vector.tensor_scalar(
            follow[:, hi], s[:, hi], -1.0, neg_max_lo[:], ALU.mult, ALU.min, accum_out=neg_max[:]
        )
        v_banks.append(pick_values(1, True, "scores"))
        os_bank = ps.tile([P, PACK, P], F32, tag="bank4")
        for t in range(PACK):
            nc.tensor.transpose(os_bank[:, t, :], os_cols[:, t : t + 1].to_broadcast([P, P]), ident[:])

        p = sb.tile([P, I], F32, tag="vals1", align_bytes=64)
        p_sum = sb.tile([P, 1], F32, tag="p_sum", align_bytes=64)
        nc.scalar.activation(p[:], s[:], ACT.Exp, bias=neg_max[:], accum_out=p_sum[:])
        v_banks.append(pick_values(2, False, "follow"))
        p_inv = sb.tile([P, 1], F32, tag="vals2", align_bytes=64)
        nc.vector.reciprocal(p_inv[:], p_sum[:])
        gain = sb.tile([P, 1], F32, tag="gain", align_bytes=64)
        nc.vector.tensor_scalar(gain[:], p_inv[:], damp_col[:], float(I), ALU.mult, ALU.mult)
        u0 = sb.tile([P, I], F32)
        u_sum = sb.tile([P, 1], F32)
        nc.scalar.activation(u0[:], p[:], ACT.Ln, bias=1.0, scale=gain[:], accum_out=u_sum[:])

        picked3 = sb.tile([P, I], BF16, tag="p_sum", align_bytes=64)
        for h in range(2):
            gather(picked3[:, slot_halves[h]], v_pool[3], list1[:, list_halves[h]], False)
        v_banks.append(turn_values(3, picked3))
        v_grouped = []
        for h, tag in enumerate(("gain", "vals1")):
            grouped = sb.tile([P, HALF, PACK], BF16, name="v_grouped%d" % h, tag=tag, align_bytes=64)
            for b in range(2):
                weave(grouped[:, b * P : (b + 1) * P, :], v_banks[2 * h + b], True)
            v_grouped.append(grouped)

        table_warm_up = sb.tile([P, 1], F32)
        nc.scalar.activation(table_warm_up[:], v_grouped[1][:, HALF - 1, 0:1], ACT.Sigmoid)
        u_inv = sb.tile([P, 1], F32, tag="vals3", align_bytes=64)
        nc.vector.reciprocal(u_inv[:], u_sum[:])
        w_bank = ps.tile([P, 2, P], F32, tag="bank5")
        for u in range(2):
            places = slice(2 * u, 2 * u + 2)
            wo = sb.tile([P, P, 2], BF16, name="wo%d" % u)
            nc.vector.scalar_tensor_tensor(
                wo[:],
                u0[:].rearrange("p (s t) -> p s t", t=PACK)[:, :, places],
                u_inv[:],
                os_bank[:, places, :].rearrange("p t s -> p s t"),
                ALU.mult,
                ALU.mult,
            )
            nc.tensor.transpose(w_bank[:, u, :], wo[:].rearrange("p s j -> p (s j)").bitcast(F32), ident[:])
        v_codes = sb.tile([P, E], U32, tag="vals3", align_bytes=64)
        v_scales = sb.tile([P, E], U8, align_bytes=64)
        quantize_values(0, v_grouped[0])
        quantize_values(1, v_grouped[1])
        w_grouped = sb.tile([P, Q, PACK], BF16, align_bytes=64)
        weave(w_grouped[:], w_bank, False)
        w_codes = sb.tile([P, Q], U32, align_bytes=64)
        w_scales = sb.tile([P, Q], U8, align_bytes=64)
        nc.vector.quantize_mx(
            out=w_codes[:].bitcast(FP8X4), scales=w_scales[:], in_=w_grouped[:].rearrange("p w j -> p (w j)")
        )

        df = sb.tile([P, E], F32)
        for h in range(2):
            cols = slice(h * HALF, (h + 1) * HALF)
            o_bank = ps.tile([P, HALF], F32, name="o_bank%d" % h, tag="bank%d" % (6 + h))
            nc.tensor.matmul_mx(
                out=o_bank[:],
                lhsT=w_codes[:].bitcast(FP8X4),
                lhsT_scale=w_scales[:],
                rhs=v_codes[:, cols].bitcast(FP8X4),
                rhs_scale=v_scales[:, cols],
                start=True,
                stop=True,
            )
            nc.vector.tensor_tensor(df[:, cols], o_bank[:], before_sb[:, cols], ALU.subtract)
        sq = sb.tile([P, E], F32)
        sq_lo = sb.tile([P, 1], F32)
        nc.scalar.activation(sq[:, :HALF], df[:, :HALF], ACT.Square, accum_out=sq_lo[:])
        sq_hi = sb.tile([P, 1], F32)
        nc.scalar.activation(sq[:, HALF:], df[:, HALF:], ACT.Square, accum_out=sq_hi[:])
        gate_bias = sb.tile([P, 1], F32)
        nc.vector.tensor_scalar(gate_bias[:], sq_lo[:], eager_mean[:], -1.0, ALU.mult, ALU.add)
        gate = sb.tile([P, 1], F32)
        nc.scalar.activation(gate[:], sq_hi[:], ACT.Sigmoid, bias=gate_bias[:], scale=eager_mean[:])
        y = sb.tile([P, E], F32)
        for h in range(2):
            cols = slice(h * HALF, (h + 1) * HALF)
            nc.vector.scalar_tensor_tensor(y[:, cols], df[:, cols], gate[:], before_sb[:, cols], ALU.mult, ALU.add)
            (nc.sync, nc.scalar)[h].dma_start(out[:, cols], y[:, cols])
